import numpy as np
import ml_dtypes


def mxq(x, axis, fmt="e4m3"):
    dtype, down = {"e4m3": (ml_dtypes.float8_e4m3fn, 7), "e5m2": (ml_dtypes.float8_e5m2, 14)}[fmt]
    v = np.moveaxis(np.asarray(x, np.float32).astype(ml_dtypes.bfloat16).astype(np.float64), axis, -1)
    blocks = v.reshape(v.shape[:-1] + (-1, 32))
    amax = np.abs(blocks).max(-1, keepdims=True)
    byte = np.maximum(np.where(amax > 0, np.frexp(amax)[1] - 1 + 127, 0) - down, 1)
    scale = np.exp2(byte - 127.0)
    codes = (blocks / scale).astype(np.float32).astype(dtype).astype(np.float64)
    return np.moveaxis((codes * scale).reshape(v.shape), -1, axis)


WIDE = False


def mx_kscale(k):
    if not WIDE:
        return np.ones(k)
    levels = np.array([10, -10, 5, -5, 0])
    if k % 512:
        return np.exp2(np.random.permutation(np.resize(levels, k // 32))).repeat(32)
    a = np.empty((k // 512, 16))
    for p in range(k // 512):
        a[p, :8] = np.random.permutation(np.resize(levels, 8))
        for g in range(8):
            far = levels[np.abs(levels - a[p, g]) >= 10]
            a[p, g + 8] = far[np.random.randint(len(far))]
    return np.exp2(a.ravel()).repeat(32)


def f64(x):
    return np.asarray(x).astype(np.float64)


def striped(idx):
    return np.tile(idx.reshape(-1, 16).T, (8, 1)).astype(np.uint16)


def unstriped(offs):
    return offs[:16].T.reshape(-1).astype(np.int64)


def striped8(idx):
    return np.concatenate([x.reshape(-1, 16).T for x in idx]).astype(np.uint16)


def runs(offs, k):
    lists = np.stack([offs[16 * r : 16 * r + 16].T.reshape(-1) for r in range(8)]).astype(np.int64)
    return lists[np.arange(k) % 512 // 64]


def pack_weight(w):
    k, n = w.shape
    w = f64(np.asarray(w, np.float32).astype(ml_dtypes.bfloat16)).reshape(k // 32, 32, n)
    amax = np.abs(w).max(1)
    byte = np.clip(np.where(amax > 0, np.frexp(amax)[1] - 1 + 127 - 7, 1), 1, 254)
    scaled = (w * np.exp2(127.0 - byte)[:, None, :]).reshape(k, n).astype(np.float32)
    words = np.ascontiguousarray(scaled.reshape(k // 512, 128, 4, n).transpose(0, 1, 3, 2)).astype(ml_dtypes.float8_e4m3fn).view(np.uint8)
    return words, np.ascontiguousarray(byte.astype(np.uint8).reshape(k // 512, 16, n))


def unpack_weight(words, scales):
    g, p, n, _ = words.shape
    vals = np.ascontiguousarray(words).view(ml_dtypes.float8_e4m3fn).astype(np.float64) * np.repeat(np.exp2(scales.astype(np.float64) - 127.0), 8, axis=1)[..., None]
    return vals.transpose(0, 1, 3, 2).reshape(g * 512, n)


E2M1 = np.array([0.0, 0.5, 1.0, 1.5, 2.0, 3.0, 4.0, 6.0, -0.0, -0.5, -1.0, -1.5, -2.0, -3.0, -4.0, -6.0])


def pack_fp4(w):
    k, n = w.shape
    w = f64(np.asarray(w, np.float32).astype(ml_dtypes.bfloat16)).reshape(k // 32, 32, n)
    amax = np.abs(w).max(1)
    mant, ex = np.frexp(amax / 6.0)
    byte = np.clip(np.where(amax > 0, np.where(mant > 0.5, ex, ex - 1) + 127, 1), 1, 254)
    scaled = (w * np.exp2(127.0 - byte)[:, None, :]).reshape(k, n).astype(np.float32)
    c = np.ascontiguousarray(scaled.reshape(k // 512, 128, 4, n).transpose(0, 1, 3, 2)).astype(ml_dtypes.float4_e2m1fn).view(np.uint8) & 0xF
    words = (c[..., 0::2] | (c[..., 1::2] << 4)).reshape(k // 512, 128, 2 * n)
    return np.ascontiguousarray(words), np.ascontiguousarray(byte.astype(np.uint8).reshape(k // 512, 16, n))


def unpack_fp4(words, scales):
    g, _, n = scales.shape
    words = np.ascontiguousarray(words).reshape(g, 128, n, 2)
    nib = np.empty((g, 128, n, 4), np.uint8)
    nib[..., 0::2] = words & 0xF
    nib[..., 1::2] = words >> 4
    vals = E2M1[nib] * np.repeat(np.exp2(scales.astype(np.float64) - 127.0), 8, axis=1)[..., None]
    return vals.transpose(0, 1, 3, 2).reshape(g * 512, n)


def sigmoid(v):
    return 1.0 / (1.0 + np.exp(-np.maximum(v, -700.0)))

def planes(y):
    n, m = y.shape
    v = y.astype(np.float32).astype(ml_dtypes.bfloat16).astype(np.float64).reshape(n // 32, 32, m)
    top = np.abs(v).max(1)
    byte = np.clip(np.where(top > 0, np.frexp(top)[1] - 1 + 127 - 7, 1), 1, 254)
    codes = (v * np.exp2(127.0 - byte)[:, None, :]).reshape(n, m).astype(np.float32).astype(ml_dtypes.float8_e4m3fn).view(np.uint8)
    words = codes.reshape(n // 512, 128, 4, m).transpose(0, 1, 3, 2)
    return np.ascontiguousarray(words), np.ascontiguousarray(byte.astype(np.uint8).reshape(n // 512, 16, m))


K, T, S, N, H = 512, 2048, 256, 512, 512


def setup_inputs():
    n = np.random.standard_normal
    s = mx_kscale(K)[:, None]
    u = mx_kscale(H)
    packed_xT = pack_weight(n((K, T)) * s)
    packed_w1 = pack_fp4(n((K, H)) / np.sqrt(K) / s)
    packed_w2 = pack_fp4(n((H, N)) / np.sqrt(H) / u[:, None])
    packed_w3 = pack_fp4(n((H, N)) / np.sqrt(H) / u[:, None])
    return {
        "x_words": packed_xT[0],
        "x_scales": packed_xT[1],
        "w1_words": packed_w1[0],
        "w1_scales": packed_w1[1],
        "gn": (np.random.uniform(0.5, 1.5, (H, 1)) * u[:, None]).astype(np.float32),
        "w2_words": packed_w2[0],
        "w2_scales": packed_w2[1],
        "gm": (np.random.uniform(0.5, 1.5, (H, 1)) * u[:, None]).astype(np.float32),
        "w3_words": packed_w3[0],
        "w3_scales": packed_w3[1],
        "offs": striped(np.random.permutation(T)[:S]),
        "n1": striped(np.random.permutation(S)),
        "n2": striped(np.random.permutation(S)),
        "n3": striped(np.random.permutation(S)),
        "n4": striped8(np.stack([np.random.permutation(S) for _ in range(8)])),
        "n5": striped(np.random.permutation(S)),
        "n6": striped(np.random.permutation(S)),
        "n7": striped(np.random.permutation(S)),
        "n8": striped(np.random.permutation(S)),
    }


def reference(x_words, x_scales, w1_words, w1_scales, gn, w2_words, w2_scales, gm, w3_words, w3_scales, offs, n1, n2, n3, n4, n5, n6, n7, n8):
    xq = unpack_weight(x_words, x_scales)[:, unstriped(offs)]
    y = unpack_fp4(w1_words, w1_scales).T @ xq
    pa = y[:, unstriped(n1)]
    z = f64(gn) * (pa + (sigmoid(y[:, unstriped(n2)])) * (y[:, unstriped(n3)] - pa))
    a = unpack_fp4(w2_words, w2_scales).T @ mxq(z, 0, "e4m3")
    z2 = f64(gm) * (np.maximum(y, y[np.arange(H)[:, None], runs(n4, H)]))
    b = unpack_fp4(w3_words, w3_scales).T @ mxq(z2, 0, "e4m3")
    out_0 = np.maximum(a[:, unstriped(n5)] + b[:, unstriped(n7)], a[:, unstriped(n6)] + b[:, unstriped(n8)])
    return (out_0,) + planes(out_0)

@@ -1,0 +1,223 @@
+from contextlib import ExitStack
+
+import concourse.mybir as mybir
+
+K, T, S, H, N = 512, 2048, 256, 512, 512
+FLOPS = 2 * S * (K * H + 2 * H * N)
+
+F32 = mybir.dt.float32
+BF16 = mybir.dt.bfloat16
+I32 = mybir.dt.int32
+U32 = mybir.dt.uint32
+U16 = mybir.dt.uint16
+U8 = mybir.dt.uint8
+FP8X4 = mybir.dt.float8_e4m3fn_x4
+FP4X4 = mybir.dt.float4_e2m1fn_x4
+ALU = mybir.AluOpType
+ACT = mybir.ActivationFunctionType
+
+P = 128
+PACK = 4
+QUADS = 4
+LIST_COLS = S // 16
+Y_WINDOW = 2 * S
+AB_WINDOW = S + 16
+RING = 2 * PACK
+SLICES = ((0, 128), (128, 256))
+
+
+def tile_picked_forkpathblerpbig_none_po_kernel(
+    tc, x_words, x_scales, w1_words, w1_scales, gn, w2_words, w2_scales, gm, w3_words, w3_scales,
+    offs, n1, n2, n3, n4, n5, n6, n7, n8, out_0, out_1, out_2,
+):
+    nc = tc.nc
+    with ExitStack() as ctx:
+        keep = ctx.enter_context(tc.tile_pool(name="keep", bufs=1))
+        psum = ctx.enter_context(tc.psum_pool(name="psum", bufs=8))
+
+        def sbuf(name, shape, dtype, tag=None):
+            return keep.tile(shape, dtype, name=name, tag=tag or name, align_bytes=64)
+
+        def load_list(name, dram):
+            tile = keep.tile([P, LIST_COLS], U16, name=name)
+            nc.sync.dma_start(tile[:], dram)
+            return tile
+
+        def load_scale_rows(name, dram, zeroing_engine):
+            tile = sbuf(name, [P, dram.shape[2]], U8)
+            zeroing_engine.memset(tile[:].bitcast(I32), 0)
+            for q in range(QUADS):
+                nc.sync.dma_start(tile[32 * q : 32 * q + 4, :].bitcast(I32), dram[0, 4 * q : 4 * q + 4, :].bitcast(I32))
+            return tile
+
+        def load_fp4_words(name, dram, queue):
+            tile = sbuf(name, [P, dram.shape[2]], U8)
+            queue.dma_start(tile[:].bitcast(I32), dram[0].bitcast(I32))
+            return tile
+
+        def load_gain(name, dram):
+            tile = sbuf(name, [P, PACK], F32)
+            nc.sync.dma_start(tile[:], dram.rearrange("(p t) o -> p (t o)", t=PACK))
+            return tile
+
+        def deal_scales(name, raw):
+            dealt = sbuf(name, [P, 512], U8, tag="dealt_scales")
+            nc.vector.tensor_copy(dealt[:].rearrange("p (t m) -> p t m", t=PACK), raw[:].rearrange("p (m t) -> p t m", t=PACK))
+            return dealt
+
+        def deal_words(name, raw):
+            dealt = sbuf(name, [P, 1024], U8)
+            nc.scalar.copy(
+                dealt[:].bitcast(U16).rearrange("p (t m) -> p t m", t=PACK),
+                raw[:].bitcast(U16).rearrange("p (m t) -> p t m", t=PACK),
+            )
+            return dealt
+
+        def deal_words_on_vector(name, raw):
+            dealt = sbuf(name, [P, 1024], U8, tag="w3_dealt")
+            nc.vector.tensor_copy(
+                dealt[:].rearrange("p (t m b) -> p t m b", t=PACK, b=2), raw[:].rearrange("p (m t b) -> p t m b", t=PACK, b=2)
+            )
+            return dealt
+
+        def window(name, width):
+            tile = sbuf(name, [P, width], F32)
+            nc.gpsimd.memset(tile[:, S:width], 0.0)
+            return tile
+
+        def product(windows, w_words, w_scales, codes, scales):
+            for t in range(PACK):
+                acc = psum.tile([P, S], F32, name="acc")
+                nc.tensor.matmul_mx(
+                    acc[:],
+                    lhsT=w_words[:, 2 * P * t : 2 * P * (t + 1)].bitcast(FP4X4),
+                    lhsT_scale=w_scales[:, P * t : P * (t + 1)],
+                    rhs=codes[:].bitcast(FP8X4),
+                    rhs_scale=scales[:],
+                    start=True,
+                    stop=True,
+                )
+                nc.vector.tensor_copy(windows[t][:, 0:S], acc[:])
+
+        def look_up(name, win, offsets, func=ACT.Copy, c0=0, c1=S, tag=None):
+            got = sbuf(name, [P, c1 - c0], F32, tag)
+            nc.scalar.activation(got[:], win[:].indirect(offsets[:, c0 // 16 : c1 // 16]), func)
+            return got
+
+        def quantize(name, planes, codes, scales, tag=None):
+            width = codes.shape[1]
+            grouped = sbuf(name, [P, width, PACK], BF16, tag)
+            nc.vector.tensor_copy(
+                grouped[:].rearrange("p (c i) t -> p c t i", i=4), planes.rearrange("p t (c i) -> p c t i", i=4)
+            )
+            nc.vector.quantize_mx(codes.bitcast(FP8X4), scales, grouped[:].rearrange("p c t -> p (c t)"))
+
+        def mx_tiles(name):
+            return sbuf(name + "_codes", [P, S], U32), sbuf(name + "_scales", [P, S], U8)
+
+        x_table = sbuf("x_table", [P, T], U32)
+        nc.scalar.dma_start(x_table[:].bitcast(I32), x_words[0].rearrange("p c r -> p (c r)").bitcast(I32))
+        offs_sb = load_list("offs_sb", offs)
+        w1_raw = load_fp4_words("w1_raw", w1_words, nc.sync)
+        xs_table = load_scale_rows("xs_table", x_scales, nc.vector)
+        w1s_raw = load_scale_rows("w1s_raw", w1_scales, nc.gpsimd)
+        w3_raw = load_fp4_words("w3_raw", w3_words, nc.sync)
+        n2_sb = load_list("n2_sb", n2)
+        n4_sb = load_list("n4_sb", n4)
+        gm_sb = load_gain("gm_sb", gm)
+        n1_sb = load_list("n1_sb", n1)
+        n3_sb = load_list("n3_sb", n3)
+        w3s_raw = load_scale_rows("w3s_raw", w3_scales, nc.gpsimd)
+        gn_sb = load_gain("gn_sb", gn)
+        w2_raw = load_fp4_words("w2_raw", w2_words, nc.sync)
+        w2s_raw = load_scale_rows("w2s_raw", w2_scales, nc.gpsimd)
+        n7_sb = load_list("n7_sb", n7)
+        n8_sb = load_list("n8_sb", n8)
+        n5_sb = load_list("n5_sb", n5)
+        n6_sb = load_list("n6_sb", n6)
+
+        y = [window("y%d" % t, Y_WINDOW) for t in range(PACK)]
+        b = [window("b%d" % t, AB_WINDOW) for t in range(PACK)]
+        a = [window("a%d" % t, AB_WINDOW) for t in range(PACK)]
+
+        w1_dealt = deal_words("w1_dealt", w1_raw)
+        w3_dealt = deal_words("w3_dealt", w3_raw)
+        picked_scales = sbuf("picked_scales", [P, S], U8)
+        nc.vector.tensor_copy(picked_scales[:], xs_table[:].indirect(offs_sb[:]))
+        w1s_dealt = deal_scales("w1s_dealt", w1s_raw)
+        picked_words = sbuf("picked_words", [P, S], U32)
+        nc.vector.tensor_copy(picked_words[:], x_table[:].indirect(offs_sb[:]))
+        product(y, w1_dealt, w1s_dealt, picked_words, picked_scales)
+
+        taken = []
+
+        def ring():
+            taken.append(len(taken) % RING)
+            return "ring%d" % taken[-1]
+
+        gate = [look_up("gate0", y[0], n2_sb, ACT.Sigmoid)]
+        z2 = sbuf("z2", [P, PACK, S], BF16)
+        for t in range(PACK):
+            other = look_up("other%d" % t, y[t], n4_sb, tag=ring())
+            larger = sbuf("larger%d" % t, [P, S], F32, tag=ring())
+            nc.vector.tensor_tensor(larger[:], y[t][:, 0:S], other[:], ALU.max)
+            nc.vector.tensor_scalar(z2[:, t, :], larger[:], gm_sb[:, t : t + 1], None, ALU.mult)
+        w3s_dealt = deal_scales("w3s_dealt", w3s_raw)
+        z2_codes, z2_scales = mx_tiles("z2")
+        quantize("z2_grouped", z2[:], z2_codes[:], z2_scales[:], tag="scratch")
+        product(b, w3_dealt, w3s_dealt, z2_codes, z2_scales)
+
+        w2_dealt = deal_words_on_vector("w2_dealt", w2_raw)
+        w2s_dealt = deal_scales("w2s_dealt", w2s_raw)
+        z = sbuf("z", [P, PACK, S], BF16)
+        for t in range(PACK):
+            pa = look_up("pa%d" % t, y[t], n1_sb, tag=ring())
+            far = look_up("far%d" % t, y[t], n3_sb, tag=ring())
+            if t > 0:
+                gate.append(look_up("gate%d" % t, y[t], n2_sb, ACT.Sigmoid, tag=ring()))
+            step = sbuf("step%d" % t, [P, S], F32, tag="scratch" if t == 2 else None)
+            nc.vector.tensor_tensor(step[:], far[:], pa[:], ALU.subtract)
+            pull = sbuf("pull%d" % t, [P, S], F32)
+            nc.vector.scalar_tensor_tensor(pull[:], step[:], gn_sb[:, t : t + 1], gate[t][:], ALU.mult, ALU.mult)
+            nc.vector.scalar_tensor_tensor(z[:, t, :], pa[:], gn_sb[:, t : t + 1], pull[:], ALU.mult, ALU.add)
+        z_codes, z_scales = mx_tiles("z")
+        quantize("z_grouped", z[:], z_codes[:], z_scales[:])
+        product(a, w2_dealt, w2s_dealt, z_codes, z_scales)
+
+        out_rows = out_0.rearrange("(p t) c -> p t c", t=PACK)
+        out_codes = out_1[0].rearrange("p c r -> p (c r)").bitcast(I32)
+        result = sbuf("result", [P, PACK, S], F32)
+        codes, scales = mx_tiles("out")
+        last = PACK - 1
+
+        def add(name, left, right):
+            total = sbuf(name, [P, left.shape[1]], F32)
+            nc.vector.tensor_tensor(total[:], left, right, ALU.add)
+            return total
+
+        b7 = []
+        b8 = []
+        for t in range(last):
+            b7.append(look_up("b7_%d" % t, b[t], n7_sb))
+            b8.append(look_up("b8_%d" % t, b[t], n8_sb))
+        for t in range(last):
+            a5 = look_up("a5_%d" % t, a[t], n5_sb)
+            a6 = look_up("a6_%d" % t, a[t], n6_sb)
+            first = add("first%d" % t, a5[:], b7[t][:])
+            second = add("second%d" % t, a6[:], b8[t][:])
+            nc.vector.tensor_tensor(result[:, t, :], first[:], second[:], ALU.max)
+            nc.sync.dma_start(out_rows[:, t, :], result[:, t, :])
+        b7_last = look_up("b7_last", b[last], n7_sb)
+        a5_last = look_up("a5_last", a[last], n5_sb)
+        b8_last = look_up("b8_last", b[last], n8_sb, tag="b8_0")
+        first = add("first_last", a5_last[:], b7_last[:])
+        for c0, c1 in SLICES:
+            a6 = look_up("a6_last%d" % c0, a[last], n6_sb, c0=c0, c1=c1)
+            second = add("second_last%d" % c0, a6[:], b8_last[:, c0:c1])
+            nc.vector.tensor_tensor(result[:, last, c0:c1], first[:, c0:c1], second[:], ALU.max)
+            nc.sync.dma_start(out_rows[:, last, c0:c1], result[:, last, c0:c1])
+            quantize("out_grouped%d" % c0, result[:, :, c0:c1], codes[:, c0:c1], scales[:, c0:c1])
+            nc.sync.dma_start(out_codes[:, c0:c1], codes[:, c0:c1].bitcast(I32))
+        for q in range(QUADS):
+            queue = nc.sync if q % 2 else nc.scalar
+            queue.dma_start(out_2[0, 4 * q : 4 * q + 4, :].bitcast(I32), scales[32 * q : 32 * q + 4, :].bitcast(I32))

@@ -118,6 +118,12 @@ def tile_picked_forkpathblerpbig_none_po_kernel(
         x_table = sbuf("x_table", [P, T], U32)
         nc.scalar.dma_start(x_table[:].bitcast(I32), x_words[0].rearrange("p c r -> p (c r)").bitcast(I32))
         offs_sb = load_list("offs_sb", offs)
+
+        warm_in = sbuf("warm_in", [P, 1], F32)
+        nc.gpsimd.memset(warm_in[:], 0.0)
+        warm_out = sbuf("warm_out", [P, 1], F32)
+        nc.scalar.activation(warm_out[:], warm_in[:], ACT.Sigmoid)
+
         w1_raw = load_fp4_words("w1_raw", w1_words, nc.sync)
         xs_table = load_scale_rows("xs_table", x_scales, nc.vector)
         w1s_raw = load_scale_rows("w1s_raw", w1_scales, nc.gpsimd)

@@ -23,6 +23,7 @@ LIST_COLS = S // 16
 Y_WINDOW = 2 * S
 AB_WINDOW = S + 16
 RING = 2 * PACK
+PLACES = {"z2": 0, "step0": 0, "step1": 0, "step2": 0, "step3": 0, "pa3": 1024, "z2_grouped": 2048, "far3": 2048, "gate3": 3072}
 SLICES = ((0, 128), (128, 256))
 
 
@@ -33,9 +34,12 @@ def tile_picked_forkpathblerpbig_none_po_kernel(
     nc = tc.nc
     with ExitStack() as ctx:
         keep = ctx.enter_context(tc.tile_pool(name="keep", bufs=1))
+        shared = ctx.enter_context(tc.tile_pool(name="shared", bufs=1))
         psum = ctx.enter_context(tc.psum_pool(name="psum", bufs=8))
 
         def sbuf(name, shape, dtype, tag=None):
+            if name in PLACES:
+                return shared.tile(shape, dtype, name=name, align_bytes=64, offset=PLACES[name])
             return keep.tile(shape, dtype, name=name, tag=tag or name, align_bytes=64)
 
         def load_list(name, dram):
@@ -43,11 +47,11 @@ def tile_picked_forkpathblerpbig_none_po_kernel(
             nc.sync.dma_start(tile[:], dram)
             return tile
 
-        def load_scale_rows(name, dram, zeroing_engine):
+        def load_scale_rows(name, dram, zeroing_engine, queues):
             tile = sbuf(name, [P, dram.shape[2]], U8)
             zeroing_engine.memset(tile[:].bitcast(I32), 0)
             for q in range(QUADS):
-                nc.sync.dma_start(tile[32 * q : 32 * q + 4, :].bitcast(I32), dram[0, 4 * q : 4 * q + 4, :].bitcast(I32))
+                queues[q].dma_start(tile[32 * q : 32 * q + 4, :].bitcast(I32), dram[0, 4 * q : 4 * q + 4, :].bitcast(I32))
             return tile
 
         def load_fp4_words(name, dram, queue):
@@ -60,8 +64,8 @@ def tile_picked_forkpathblerpbig_none_po_kernel(
             nc.sync.dma_start(tile[:], dram.rearrange("(p t) o -> p (t o)", t=PACK))
             return tile
 
-        def deal_scales(name, raw):
-            dealt = sbuf(name, [P, 512], U8, tag="dealt_scales")
+        def deal_scales(name, raw, tag=None):
+            dealt = sbuf(name, [P, 512], U8, tag=tag)
             nc.vector.tensor_copy(dealt[:].rearrange("p (t m) -> p t m", t=PACK), raw[:].rearrange("p (m t) -> p t m", t=PACK))
             return dealt
 
@@ -74,7 +78,7 @@ def tile_picked_forkpathblerpbig_none_po_kernel(
             return dealt
 
         def deal_words_on_vector(name, raw):
-            dealt = sbuf(name, [P, 1024], U8, tag="w3_dealt")
+            dealt = sbuf(name, [P, 1024], U8, tag="dealt_words")
             nc.vector.tensor_copy(
                 dealt[:].rearrange("p (t m b) -> p t m b", t=PACK, b=2), raw[:].rearrange("p (m t b) -> p t m b", t=PACK, b=2)
             )
@@ -82,7 +86,7 @@ def tile_picked_forkpathblerpbig_none_po_kernel(
 
         def window(name, width):
             tile = sbuf(name, [P, width], F32)
-            nc.gpsimd.memset(tile[:, S:width], 0.0)
+            nc.vector.memset(tile[:, S:width], 0.0)
             return tile
 
         def product(windows, w_words, w_scales, codes, scales):
@@ -115,28 +119,28 @@ def tile_picked_forkpathblerpbig_none_po_kernel(
         def mx_tiles(name):
             return sbuf(name + "_codes", [P, S], U32), sbuf(name + "_scales", [P, S], U8)
 
-        x_table = sbuf("x_table", [P, T], U32)
-        nc.scalar.dma_start(x_table[:].bitcast(I32), x_words[0].rearrange("p c r -> p (c r)").bitcast(I32))
         offs_sb = load_list("offs_sb", offs)
+        w1_raw = load_fp4_words("w1_raw", w1_words, nc.scalar)
+        x_table = sbuf("x_table", [P, T], U32)
+        nc.sync.dma_start(x_table[:].bitcast(I32), x_words[0].rearrange("p c r -> p (c r)").bitcast(I32))
+        w3_raw = load_fp4_words("w3_raw", w3_words, nc.sync)
+        xs_table = load_scale_rows("xs_table", x_scales, nc.vector, [nc.scalar] * QUADS)
+        w1s_raw = load_scale_rows("w1s_raw", w1_scales, nc.gpsimd, [nc.gpsimd, nc.gpsimd, nc.scalar, nc.scalar])
 
         warm_in = sbuf("warm_in", [P, 1], F32)
-        nc.gpsimd.memset(warm_in[:], 0.0)
+        nc.vector.memset(warm_in[:], 0.0)
         warm_out = sbuf("warm_out", [P, 1], F32)
         nc.scalar.activation(warm_out[:], warm_in[:], ACT.Sigmoid)
 
-        w1_raw = load_fp4_words("w1_raw", w1_words, nc.sync)
-        xs_table = load_scale_rows("xs_table", x_scales, nc.vector)
-        w1s_raw = load_scale_rows("w1s_raw", w1_scales, nc.gpsimd)
-        w3_raw = load_fp4_words("w3_raw", w3_words, nc.sync)
         n2_sb = load_list("n2_sb", n2)
         n4_sb = load_list("n4_sb", n4)
         gm_sb = load_gain("gm_sb", gm)
+        w2_raw = load_fp4_words("w2_raw", w2_words, nc.sync)
+        w3s_raw = load_scale_rows("w3s_raw", w3_scales, nc.vector, [nc.sync] * QUADS)
         n1_sb = load_list("n1_sb", n1)
         n3_sb = load_list("n3_sb", n3)
-        w3s_raw = load_scale_rows("w3s_raw", w3_scales, nc.gpsimd)
+        w2s_raw = load_scale_rows("w2s_raw", w2_scales, nc.vector, [nc.sync] * QUADS)
         gn_sb = load_gain("gn_sb", gn)
-        w2_raw = load_fp4_words("w2_raw", w2_words, nc.sync)
-        w2s_raw = load_scale_rows("w2s_raw", w2_scales, nc.gpsimd)
         n7_sb = load_list("n7_sb", n7)
         n8_sb = load_list("n8_sb", n8)
         n5_sb = load_list("n5_sb", n5)
@@ -146,7 +150,7 @@ def tile_picked_forkpathblerpbig_none_po_kernel(
         b = [window("b%d" % t, AB_WINDOW) for t in range(PACK)]
         a = [window("a%d" % t, AB_WINDOW) for t in range(PACK)]
 
-        w1_dealt = deal_words("w1_dealt", w1_raw)
+        w1_dealt = deal_words_on_vector("w1_dealt", w1_raw)
         w3_dealt = deal_words("w3_dealt", w3_raw)
         picked_scales = sbuf("picked_scales", [P, S], U8)
         nc.vector.tensor_copy(picked_scales[:], xs_table[:].indirect(offs_sb[:]))
@@ -168,20 +172,20 @@ def tile_picked_forkpathblerpbig_none_po_kernel(
             larger = sbuf("larger%d" % t, [P, S], F32, tag=ring())
             nc.vector.tensor_tensor(larger[:], y[t][:, 0:S], other[:], ALU.max)
             nc.vector.tensor_scalar(z2[:, t, :], larger[:], gm_sb[:, t : t + 1], None, ALU.mult)
-        w3s_dealt = deal_scales("w3s_dealt", w3s_raw)
+        w3s_dealt = deal_scales("w3s_dealt", w3s_raw, tag="w1s_dealt")
+        w2_dealt = deal_words_on_vector("w2_dealt", w2_raw)
+        w2s_dealt = deal_scales("w2s_dealt", w2s_raw, tag="w2_raw")
         z2_codes, z2_scales = mx_tiles("z2")
-        quantize("z2_grouped", z2[:], z2_codes[:], z2_scales[:], tag="scratch")
+        quantize("z2_grouped", z2[:], z2_codes[:], z2_scales[:])
         product(b, w3_dealt, w3s_dealt, z2_codes, z2_scales)
 
-        w2_dealt = deal_words_on_vector("w2_dealt", w2_raw)
-        w2s_dealt = deal_scales("w2s_dealt", w2s_raw)
         z = sbuf("z", [P, PACK, S], BF16)
         for t in range(PACK):
             pa = look_up("pa%d" % t, y[t], n1_sb, tag=ring())
             far = look_up("far%d" % t, y[t], n3_sb, tag=ring())
             if t > 0:
                 gate.append(look_up("gate%d" % t, y[t], n2_sb, ACT.Sigmoid, tag=ring()))
-            step = sbuf("step%d" % t, [P, S], F32, tag="scratch" if t == 2 else None)
+            step = sbuf("step%d" % t, [P, S], F32)
             nc.vector.tensor_tensor(step[:], far[:], pa[:], ALU.subtract)
             pull = sbuf("pull%d" % t, [P, S], F32)
             nc.vector.scalar_tensor_tensor(pull[:], step[:], gn_sb[:, t : t + 1], gate[t][:], ALU.mult, ALU.mult)
@@ -203,9 +207,10 @@ def tile_picked_forkpathblerpbig_none_po_kernel(
 
         b7 = []
         b8 = []
-        for t in range(last):
+        for t in range(PACK):
             b7.append(look_up("b7_%d" % t, b[t], n7_sb))
-            b8.append(look_up("b8_%d" % t, b[t], n8_sb))
+            if t < last:
+                b8.append(look_up("b8_%d" % t, b[t], n8_sb))
         for t in range(last):
             a5 = look_up("a5_%d" % t, a[t], n5_sb)
             a6 = look_up("a6_%d" % t, a[t], n6_sb)
@@ -213,10 +218,9 @@ def tile_picked_forkpathblerpbig_none_po_kernel(
             second = add("second%d" % t, a6[:], b8[t][:])
             nc.vector.tensor_tensor(result[:, t, :], first[:], second[:], ALU.max)
             nc.sync.dma_start(out_rows[:, t, :], result[:, t, :])
-        b7_last = look_up("b7_last", b[last], n7_sb)
         a5_last = look_up("a5_last", a[last], n5_sb)
+        first = add("first_last", a5_last[:], b7[last][:])
         b8_last = look_up("b8_last", b[last], n8_sb, tag="b8_0")
-        first = add("first_last", a5_last[:], b7_last[:])
         for c0, c1 in SLICES:
             a6 = look_up("a6_last%d" % c0, a[last], n6_sb, c0=c0, c1=c1)
             second = add("second_last%d" % c0, a6[:], b8_last[:, c0:c1])

@@ -23,7 +23,6 @@ LIST_COLS = S // 16
 Y_WINDOW = 2 * S
 AB_WINDOW = S + 16
 RING = 2 * PACK
-PLACES = {"z2": 0, "step0": 0, "step1": 0, "step2": 0, "step3": 0, "pa3": 1024, "z2_grouped": 2048, "far3": 2048, "gate3": 3072}
 SLICES = ((0, 128), (128, 256))
 
 
@@ -34,12 +33,9 @@ def tile_picked_forkpathblerpbig_none_po_kernel(
     nc = tc.nc
     with ExitStack() as ctx:
         keep = ctx.enter_context(tc.tile_pool(name="keep", bufs=1))
-        shared = ctx.enter_context(tc.tile_pool(name="shared", bufs=1))
         psum = ctx.enter_context(tc.psum_pool(name="psum", bufs=8))
 
         def sbuf(name, shape, dtype, tag=None):
-            if name in PLACES:
-                return shared.tile(shape, dtype, name=name, align_bytes=64, offset=PLACES[name])
             return keep.tile(shape, dtype, name=name, tag=tag or name, align_bytes=64)
 
         def load_list(name, dram):
@@ -47,16 +43,16 @@ def tile_picked_forkpathblerpbig_none_po_kernel(
             nc.sync.dma_start(tile[:], dram)
             return tile
 
-        def load_scale_rows(name, dram, zeroing_engine, queues):
+        def load_scale_rows(name, dram):
             tile = sbuf(name, [P, dram.shape[2]], U8)
-            zeroing_engine.memset(tile[:].bitcast(I32), 0)
+            nc.gpsimd.memset(tile[:].bitcast(I32), 0)
             for q in range(QUADS):
-                queues[q].dma_start(tile[32 * q : 32 * q + 4, :].bitcast(I32), dram[0, 4 * q : 4 * q + 4, :].bitcast(I32))
+                nc.sync.dma_start(tile[32 * q : 32 * q + 4, :].bitcast(I32), dram[0, 4 * q : 4 * q + 4, :].bitcast(I32))
             return tile
 
-        def load_fp4_words(name, dram, queue):
+        def load_fp4_words(name, dram):
             tile = sbuf(name, [P, dram.shape[2]], U8)
-            queue.dma_start(tile[:].bitcast(I32), dram[0].bitcast(I32))
+            nc.sync.dma_start(tile[:].bitcast(I32), dram[0].bitcast(I32))
             return tile
 
         def load_gain(name, dram):
@@ -77,16 +73,9 @@ def tile_picked_forkpathblerpbig_none_po_kernel(
             )
             return dealt
 
-        def deal_words_on_vector(name, raw):
-            dealt = sbuf(name, [P, 1024], U8, tag="dealt_words")
-            nc.vector.tensor_copy(
-                dealt[:].rearrange("p (t m b) -> p t m b", t=PACK, b=2), raw[:].rearrange("p (m t b) -> p t m b", t=PACK, b=2)
-            )
-            return dealt
-
         def window(name, width):
             tile = sbuf(name, [P, width], F32)
-            nc.vector.memset(tile[:, S:width], 0.0)
+            nc.gpsimd.memset(tile[:, S:width], 0.0)
             return tile
 
         def product(windows, w_words, w_scales, codes, scales):
@@ -120,27 +109,27 @@ def tile_picked_forkpathblerpbig_none_po_kernel(
             return sbuf(name + "_codes", [P, S], U32), sbuf(name + "_scales", [P, S], U8)
 
         offs_sb = load_list("offs_sb", offs)
-        w1_raw = load_fp4_words("w1_raw", w1_words, nc.scalar)
+        w1_raw = load_fp4_words("w1_raw", w1_words)
+        w3_raw = load_fp4_words("w3_raw", w3_words)
+        xs_table = load_scale_rows("xs_table", x_scales)
         x_table = sbuf("x_table", [P, T], U32)
         nc.sync.dma_start(x_table[:].bitcast(I32), x_words[0].rearrange("p c r -> p (c r)").bitcast(I32))
-        w3_raw = load_fp4_words("w3_raw", w3_words, nc.sync)
-        xs_table = load_scale_rows("xs_table", x_scales, nc.vector, [nc.scalar] * QUADS)
-        w1s_raw = load_scale_rows("w1s_raw", w1_scales, nc.gpsimd, [nc.gpsimd, nc.gpsimd, nc.scalar, nc.scalar])
+        w1s_raw = load_scale_rows("w1s_raw", w1_scales)
 
         warm_in = sbuf("warm_in", [P, 1], F32)
         nc.vector.memset(warm_in[:], 0.0)
         warm_out = sbuf("warm_out", [P, 1], F32)
         nc.scalar.activation(warm_out[:], warm_in[:], ACT.Sigmoid)
 
+        w2_raw = load_fp4_words("w2_raw", w2_words)
         n2_sb = load_list("n2_sb", n2)
         n4_sb = load_list("n4_sb", n4)
-        gm_sb = load_gain("gm_sb", gm)
-        w2_raw = load_fp4_words("w2_raw", w2_words, nc.sync)
-        w3s_raw = load_scale_rows("w3s_raw", w3_scales, nc.vector, [nc.sync] * QUADS)
         n1_sb = load_list("n1_sb", n1)
         n3_sb = load_list("n3_sb", n3)
-        w2s_raw = load_scale_rows("w2s_raw", w2_scales, nc.vector, [nc.sync] * QUADS)
+        gm_sb = load_gain("gm_sb", gm)
         gn_sb = load_gain("gn_sb", gn)
+        w3s_raw = load_scale_rows("w3s_raw", w3_scales)
+        w2s_raw = load_scale_rows("w2s_raw", w2_scales)
         n7_sb = load_list("n7_sb", n7)
         n8_sb = load_list("n8_sb", n8)
         n5_sb = load_list("n5_sb", n5)
@@ -150,14 +139,18 @@ def tile_picked_forkpathblerpbig_none_po_kernel(
         b = [window("b%d" % t, AB_WINDOW) for t in range(PACK)]
         a = [window("a%d" % t, AB_WINDOW) for t in range(PACK)]
 
-        w1_dealt = deal_words_on_vector("w1_dealt", w1_raw)
+        w1_dealt = deal_words("w1_dealt", w1_raw)
         w3_dealt = deal_words("w3_dealt", w3_raw)
+        w2_dealt = deal_words("w2_dealt", w2_raw)
         picked_scales = sbuf("picked_scales", [P, S], U8)
         nc.vector.tensor_copy(picked_scales[:], xs_table[:].indirect(offs_sb[:]))
         w1s_dealt = deal_scales("w1s_dealt", w1s_raw)
         picked_words = sbuf("picked_words", [P, S], U32)
         nc.vector.tensor_copy(picked_words[:], x_table[:].indirect(offs_sb[:]))
         product(y, w1_dealt, w1s_dealt, picked_words, picked_scales)
+
+        w3s_dealt = deal_scales("w3s_dealt", w3s_raw, tag="w1s_dealt")
+        w2s_dealt = deal_scales("w2s_dealt", w2s_raw, tag="w1_dealt")
 
         taken = []
 
@@ -172,20 +165,17 @@ def tile_picked_forkpathblerpbig_none_po_kernel(
             larger = sbuf("larger%d" % t, [P, S], F32, tag=ring())
             nc.vector.tensor_tensor(larger[:], y[t][:, 0:S], other[:], ALU.max)
             nc.vector.tensor_scalar(z2[:, t, :], larger[:], gm_sb[:, t : t + 1], None, ALU.mult)
-        w3s_dealt = deal_scales("w3s_dealt", w3s_raw, tag="w1s_dealt")
-        w2_dealt = deal_words_on_vector("w2_dealt", w2_raw)
-        w2s_dealt = deal_scales("w2s_dealt", w2s_raw, tag="w2_raw")
         z2_codes, z2_scales = mx_tiles("z2")
         quantize("z2_grouped", z2[:], z2_codes[:], z2_scales[:])
         product(b, w3_dealt, w3s_dealt, z2_codes, z2_scales)
 
         z = sbuf("z", [P, PACK, S], BF16)
         for t in range(PACK):
-            pa = look_up("pa%d" % t, y[t], n1_sb, tag=ring())
-            far = look_up("far%d" % t, y[t], n3_sb, tag=ring())
+            pa = look_up("pa%d" % t, y[t], n1_sb, tag=ring() if t < 3 else "ring1")
+            far = look_up("far%d" % t, y[t], n3_sb, tag=ring() if t < 3 else "gate0")
             if t > 0:
-                gate.append(look_up("gate%d" % t, y[t], n2_sb, ACT.Sigmoid, tag=ring()))
-            step = sbuf("step%d" % t, [P, S], F32)
+                gate.append(look_up("gate%d" % t, y[t], n2_sb, ACT.Sigmoid, tag=ring() if t < 3 else "z2_grouped"))
+            step = sbuf("step%d" % t, [P, S], F32, tag="z2")
             nc.vector.tensor_tensor(step[:], far[:], pa[:], ALU.subtract)
             pull = sbuf("pull%d" % t, [P, S], F32)
             nc.vector.scalar_tensor_tensor(pull[:], step[:], gn_sb[:, t : t + 1], gate[t][:], ALU.mult, ALU.mult)

@@ -18,12 +18,14 @@ ACT = mybir.ActivationFunctionType
 
 P = 128
 PACK = 4
+LAST = PACK - 1
 QUADS = 4
-LIST_COLS = S // 16
+PSUM_BANKS = 8
+LIST_ROWS = 16
 Y_WINDOW = 2 * S
-AB_WINDOW = S + 16
+AB_WINDOW = S + LIST_ROWS
 RING = 2 * PACK
-SLICES = ((0, 128), (128, 256))
+HALVES = ((0, S // 2), (S // 2, S))
 
 
 def tile_picked_forkpathblerpbig_none_po_kernel(
@@ -33,13 +35,13 @@ def tile_picked_forkpathblerpbig_none_po_kernel(
     nc = tc.nc
     with ExitStack() as ctx:
         keep = ctx.enter_context(tc.tile_pool(name="keep", bufs=1))
-        psum = ctx.enter_context(tc.psum_pool(name="psum", bufs=8))
+        psum = ctx.enter_context(tc.psum_pool(name="psum", bufs=PSUM_BANKS))
 
         def sbuf(name, shape, dtype, tag=None):
             return keep.tile(shape, dtype, name=name, tag=tag or name, align_bytes=64)
 
         def load_list(name, dram):
-            tile = keep.tile([P, LIST_COLS], U16, name=name)
+            tile = keep.tile([P, S // LIST_ROWS], U16, name=name)
             nc.sync.dma_start(tile[:], dram)
             return tile
 
@@ -60,13 +62,17 @@ def tile_picked_forkpathblerpbig_none_po_kernel(
             nc.sync.dma_start(tile[:], dram.rearrange("(p t) o -> p (t o)", t=PACK))
             return tile
 
-        def deal_scales(name, raw, tag=None):
-            dealt = sbuf(name, [P, 512], U8, tag=tag)
-            nc.vector.tensor_copy(dealt[:].rearrange("p (t m) -> p t m", t=PACK), raw[:].rearrange("p (m t) -> p t m", t=PACK))
+        def deal_scales(name, raw, pieces, tag=None):
+            dealt = sbuf(name, [P, PACK * P], U8, tag=tag)
+            for t0, t1 in pieces:
+                nc.vector.tensor_copy(
+                    dealt[:].rearrange("p (t m) -> p t m", t=PACK)[:, t0:t1, :],
+                    raw[:].rearrange("p (m t) -> p t m", t=PACK)[:, t0:t1, :],
+                )
             return dealt
 
         def deal_words(name, raw):
-            dealt = sbuf(name, [P, 1024], U8)
+            dealt = sbuf(name, [P, 2 * PACK * P], U8)
             nc.scalar.copy(
                 dealt[:].bitcast(U16).rearrange("p (t m) -> p t m", t=PACK),
                 raw[:].bitcast(U16).rearrange("p (m t) -> p t m", t=PACK),
@@ -94,19 +100,24 @@ def tile_picked_forkpathblerpbig_none_po_kernel(
 
         def look_up(name, win, offsets, func=ACT.Copy, c0=0, c1=S, tag=None):
             got = sbuf(name, [P, c1 - c0], F32, tag)
-            nc.scalar.activation(got[:], win[:].indirect(offsets[:, c0 // 16 : c1 // 16]), func)
+            nc.scalar.activation(got[:], win[:].indirect(offsets[:, c0 // LIST_ROWS : c1 // LIST_ROWS]), func)
             return got
 
-        def quantize(name, planes, codes, scales, tag=None):
+        def quantize(name, row_tiles, codes, scales):
             width = codes.shape[1]
-            grouped = sbuf(name, [P, width, PACK], BF16, tag)
+            grouped = sbuf(name, [P, width, PACK], BF16)
             nc.vector.tensor_copy(
-                grouped[:].rearrange("p (c i) t -> p c t i", i=4), planes.rearrange("p t (c i) -> p c t i", i=4)
+                grouped[:].rearrange("p (c i) t -> p c t i", i=4), row_tiles.rearrange("p t (c i) -> p c t i", i=4)
             )
             nc.vector.quantize_mx(codes.bitcast(FP8X4), scales, grouped[:].rearrange("p c t -> p (c t)"))
 
         def mx_tiles(name):
             return sbuf(name + "_codes", [P, S], U32), sbuf(name + "_scales", [P, S], U8)
+
+        def add(name, left, right):
+            total = sbuf(name, [P, left.shape[1]], F32)
+            nc.vector.tensor_tensor(total[:], left, right, ALU.add)
+            return total
 
         offs_sb = load_list("offs_sb", offs)
         w1_raw = load_fp4_words("w1_raw", w1_words)
@@ -144,13 +155,13 @@ def tile_picked_forkpathblerpbig_none_po_kernel(
         w2_dealt = deal_words("w2_dealt", w2_raw)
         picked_scales = sbuf("picked_scales", [P, S], U8)
         nc.vector.tensor_copy(picked_scales[:], xs_table[:].indirect(offs_sb[:]))
-        w1s_dealt = deal_scales("w1s_dealt", w1s_raw)
+        w1s_dealt = deal_scales("w1s_dealt", w1s_raw, ((0, 1), (1, PACK)))
         picked_words = sbuf("picked_words", [P, S], U32)
         nc.vector.tensor_copy(picked_words[:], x_table[:].indirect(offs_sb[:]))
         product(y, w1_dealt, w1s_dealt, picked_words, picked_scales)
 
-        w3s_dealt = deal_scales("w3s_dealt", w3s_raw, tag="w1s_dealt")
-        w2s_dealt = deal_scales("w2s_dealt", w2s_raw, tag="w1_dealt")
+        w3s_dealt = deal_scales("w3s_dealt", w3s_raw, ((0, PACK),), tag="w1s_dealt")
+        w2s_dealt = deal_scales("w2s_dealt", w2s_raw, ((0, PACK),), tag="w1_dealt")
 
         taken = []
 
@@ -171,10 +182,10 @@ def tile_picked_forkpathblerpbig_none_po_kernel(
 
         z = sbuf("z", [P, PACK, S], BF16)
         for t in range(PACK):
-            pa = look_up("pa%d" % t, y[t], n1_sb, tag=ring() if t < 3 else "ring1")
-            far = look_up("far%d" % t, y[t], n3_sb, tag=ring() if t < 3 else "gate0")
+            pa = look_up("pa%d" % t, y[t], n1_sb, tag=ring() if t < LAST else "ring1")
+            far = look_up("far%d" % t, y[t], n3_sb, tag=ring() if t < LAST else "z2_grouped")
             if t > 0:
-                gate.append(look_up("gate%d" % t, y[t], n2_sb, ACT.Sigmoid, tag=ring() if t < 3 else "z2_grouped"))
+                gate.append(look_up("gate%d" % t, y[t], n2_sb, ACT.Sigmoid, tag=ring() if t < LAST else "gate0"))
             step = sbuf("step%d" % t, [P, S], F32, tag="z2")
             nc.vector.tensor_tensor(step[:], far[:], pa[:], ALU.subtract)
             pull = sbuf("pull%d" % t, [P, S], F32)
@@ -188,34 +199,25 @@ def tile_picked_forkpathblerpbig_none_po_kernel(
         out_codes = out_1[0].rearrange("p c r -> p (c r)").bitcast(I32)
         result = sbuf("result", [P, PACK, S], F32)
         codes, scales = mx_tiles("out")
-        last = PACK - 1
-
-        def add(name, left, right):
-            total = sbuf(name, [P, left.shape[1]], F32)
-            nc.vector.tensor_tensor(total[:], left, right, ALU.add)
-            return total
-
         b7 = []
         b8 = []
         for t in range(PACK):
             b7.append(look_up("b7_%d" % t, b[t], n7_sb))
-            if t < last:
-                b8.append(look_up("b8_%d" % t, b[t], n8_sb))
-        for t in range(last):
+            b8.append(look_up("b8_%d" % t, b[t], n8_sb))
+        for t in range(LAST):
             a5 = look_up("a5_%d" % t, a[t], n5_sb)
             a6 = look_up("a6_%d" % t, a[t], n6_sb)
             first = add("first%d" % t, a5[:], b7[t][:])
             second = add("second%d" % t, a6[:], b8[t][:])
             nc.vector.tensor_tensor(result[:, t, :], first[:], second[:], ALU.max)
             nc.sync.dma_start(out_rows[:, t, :], result[:, t, :])
-        a5_last = look_up("a5_last", a[last], n5_sb)
-        first = add("first_last", a5_last[:], b7[last][:])
-        b8_last = look_up("b8_last", b[last], n8_sb, tag="b8_0")
-        for c0, c1 in SLICES:
-            a6 = look_up("a6_last%d" % c0, a[last], n6_sb, c0=c0, c1=c1)
-            second = add("second_last%d" % c0, a6[:], b8_last[:, c0:c1])
-            nc.vector.tensor_tensor(result[:, last, c0:c1], first[:, c0:c1], second[:], ALU.max)
-            nc.sync.dma_start(out_rows[:, last, c0:c1], result[:, last, c0:c1])
+        a5 = look_up("a5_last", a[LAST], n5_sb)
+        first = add("first_last", a5[:], b7[LAST][:])
+        for c0, c1 in HALVES:
+            a6 = look_up("a6_last%d" % c0, a[LAST], n6_sb, c0=c0, c1=c1)
+            second = add("second_last%d" % c0, a6[:], b8[LAST][:, c0:c1])
+            nc.vector.tensor_tensor(result[:, LAST, c0:c1], first[:, c0:c1], second[:], ALU.max)
+            nc.sync.dma_start(out_rows[:, LAST, c0:c1], result[:, LAST, c0:c1])
             quantize("out_grouped%d" % c0, result[:, :, c0:c1], codes[:, c0:c1], scales[:, c0:c1])
             nc.sync.dma_start(out_codes[:, c0:c1], codes[:, c0:c1].bitcast(I32))
         for q in range(QUADS):

from contextlib import ExitStack

import concourse.mybir as mybir

K, T, S, H, N = 512, 2048, 256, 512, 512
FLOPS = 2 * S * (K * H + 2 * H * N)

F32 = mybir.dt.float32
BF16 = mybir.dt.bfloat16
I32 = mybir.dt.int32
U32 = mybir.dt.uint32
U16 = mybir.dt.uint16
U8 = mybir.dt.uint8
FP8X4 = mybir.dt.float8_e4m3fn_x4
FP4X4 = mybir.dt.float4_e2m1fn_x4
ALU = mybir.AluOpType
ACT = mybir.ActivationFunctionType

P = 128
PACK = 4
LAST = PACK - 1
QUADS = 4
PSUM_BANKS = 8
LIST_ROWS = 16
Y_WINDOW = 2 * S
AB_WINDOW = S + LIST_ROWS
RING = 2 * PACK
HALVES = ((0, S // 2), (S // 2, S))


def tile_picked_forkpathblerpbig_none_po_kernel(
    tc, x_words, x_scales, w1_words, w1_scales, gn, w2_words, w2_scales, gm, w3_words, w3_scales,
    offs, n1, n2, n3, n4, n5, n6, n7, n8, out_0, out_1, out_2,
):
    nc = tc.nc
    with ExitStack() as ctx:
        keep = ctx.enter_context(tc.tile_pool(name="keep", bufs=1))
        psum = ctx.enter_context(tc.psum_pool(name="psum", bufs=PSUM_BANKS))

        def sbuf(name, shape, dtype, tag=None):
            return keep.tile(shape, dtype, name=name, tag=tag or name, align_bytes=64)

        def load_list(name, dram):
            tile = keep.tile([P, S // LIST_ROWS], U16, name=name)
            nc.sync.dma_start(tile[:], dram)
            return tile

        def load_scale_rows(name, dram):
            tile = sbuf(name, [P, dram.shape[2]], U8)
            nc.gpsimd.memset(tile[:].bitcast(I32), 0)
            for q in range(QUADS):
                nc.sync.dma_start(tile[32 * q : 32 * q + 4, :].bitcast(I32), dram[0, 4 * q : 4 * q + 4, :].bitcast(I32))
            return tile

        def load_fp4_words(name, dram):
            tile = sbuf(name, [P, dram.shape[2]], U8)
            nc.sync.dma_start(tile[:].bitcast(I32), dram[0].bitcast(I32))
            return tile

        def load_gain(name, dram):
            tile = sbuf(name, [P, PACK], F32)
            nc.sync.dma_start(tile[:], dram.rearrange("(p t) o -> p (t o)", t=PACK))
            return tile

        def deal_scales(name, raw, pieces, tag=None):
            dealt = sbuf(name, [P, PACK * P], U8, tag=tag)
            for t0, t1 in pieces:
                nc.vector.tensor_copy(
                    dealt[:].rearrange("p (t m) -> p t m", t=PACK)[:, t0:t1, :],
                    raw[:].rearrange("p (m t) -> p t m", t=PACK)[:, t0:t1, :],
                )
            return dealt

        def deal_words(name, raw):
            dealt = sbuf(name, [P, 2 * PACK * P], U8)
            nc.scalar.copy(
                dealt[:].bitcast(U16).rearrange("p (t m) -> p t m", t=PACK),
                raw[:].bitcast(U16).rearrange("p (m t) -> p t m", t=PACK),
            )
            return dealt

        def window(name, width):
            tile = sbuf(name, [P, width], F32)
            nc.gpsimd.memset(tile[:, S:width], 0.0)
            return tile

        def product(windows, w_words, w_scales, codes, scales):
            for t in range(PACK):
                acc = psum.tile([P, S], F32, name="acc")
                nc.tensor.matmul_mx(
                    acc[:],
                    lhsT=w_words[:, 2 * P * t : 2 * P * (t + 1)].bitcast(FP4X4),
                    lhsT_scale=w_scales[:, P * t : P * (t + 1)],
                    rhs=codes[:].bitcast(FP8X4),
                    rhs_scale=scales[:],
                    start=True,
                    stop=True,
                )
                nc.vector.tensor_copy(windows[t][:, 0:S], acc[:])

        def look_up(name, win, offsets, func=ACT.Copy, c0=0, c1=S, tag=None):
            got = sbuf(name, [P, c1 - c0], F32, tag)
            nc.scalar.activation(got[:], win[:].indirect(offsets[:, c0 // LIST_ROWS : c1 // LIST_ROWS]), func)
            return got

        def quantize(name, row_tiles, codes, scales):
            width = codes.shape[1]
            grouped = sbuf(name, [P, width, PACK], BF16)
            nc.vector.tensor_copy(
                grouped[:].rearrange("p (c i) t -> p c t i", i=4), row_tiles.rearrange("p t (c i) -> p c t i", i=4)
            )
            nc.vector.quantize_mx(codes.bitcast(FP8X4), scales, grouped[:].rearrange("p c t -> p (c t)"))

        def mx_tiles(name):
            return sbuf(name + "_codes", [P, S], U32), sbuf(name + "_scales", [P, S], U8)

        def add(name, left, right):
            total = sbuf(name, [P, left.shape[1]], F32)
            nc.vector.tensor_tensor(total[:], left, right, ALU.add)
            return total

        offs_sb = load_list("offs_sb", offs)
        w1_raw = load_fp4_words("w1_raw", w1_words)
        w3_raw = load_fp4_words("w3_raw", w3_words)
        xs_table = load_scale_rows("xs_table", x_scales)
        x_table = sbuf("x_table", [P, T], U32)
        nc.sync.dma_start(x_table[:].bitcast(I32), x_words[0].rearrange("p c r -> p (c r)").bitcast(I32))
        w1s_raw = load_scale_rows("w1s_raw", w1_scales)

        warm_in = sbuf("warm_in", [P, 1], F32)
        nc.vector.memset(warm_in[:], 0.0)
        warm_out = sbuf("warm_out", [P, 1], F32)
        nc.scalar.activation(warm_out[:], warm_in[:], ACT.Sigmoid)

        w2_raw = load_fp4_words("w2_raw", w2_words)
        n2_sb = load_list("n2_sb", n2)
        n4_sb = load_list("n4_sb", n4)
        n1_sb = load_list("n1_sb", n1)
        n3_sb = load_list("n3_sb", n3)
        gm_sb = load_gain("gm_sb", gm)
        gn_sb = load_gain("gn_sb", gn)
        w3s_raw = load_scale_rows("w3s_raw", w3_scales)
        w2s_raw = load_scale_rows("w2s_raw", w2_scales)
        n7_sb = load_list("n7_sb", n7)
        n8_sb = load_list("n8_sb", n8)
        n5_sb = load_list("n5_sb", n5)
        n6_sb = load_list("n6_sb", n6)

        y = [window("y%d" % t, Y_WINDOW) for t in range(PACK)]
        b = [window("b%d" % t, AB_WINDOW) for t in range(PACK)]
        a = [window("a%d" % t, AB_WINDOW) for t in range(PACK)]

        w1_dealt = deal_words("w1_dealt", w1_raw)
        w3_dealt = deal_words("w3_dealt", w3_raw)
        w2_dealt = deal_words("w2_dealt", w2_raw)
        picked_scales = sbuf("picked_scales", [P, S], U8)
        nc.vector.tensor_copy(picked_scales[:], xs_table[:].indirect(offs_sb[:]))
        w1s_dealt = deal_scales("w1s_dealt", w1s_raw, ((0, 1), (1, PACK)))
        picked_words = sbuf("picked_words", [P, S], U32)
        nc.vector.tensor_copy(picked_words[:], x_table[:].indirect(offs_sb[:]))
        product(y, w1_dealt, w1s_dealt, picked_words, picked_scales)

        w3s_dealt = deal_scales("w3s_dealt", w3s_raw, ((0, PACK),), tag="w1s_dealt")
        w2s_dealt = deal_scales("w2s_dealt", w2s_raw, ((0, PACK),), tag="w1_dealt")

        taken = []

        def ring():
            taken.append(len(taken) % RING)
            return "ring%d" % taken[-1]

        gate = [look_up("gate0", y[0], n2_sb, ACT.Sigmoid)]
        z2 = sbuf("z2", [P, PACK, S], BF16)
        for t in range(PACK):
            other = look_up("other%d" % t, y[t], n4_sb, tag=ring())
            larger = sbuf("larger%d" % t, [P, S], F32, tag=ring())
            nc.vector.tensor_tensor(larger[:], y[t][:, 0:S], other[:], ALU.max)
            nc.vector.tensor_scalar(z2[:, t, :], larger[:], gm_sb[:, t : t + 1], None, ALU.mult)
        z2_codes, z2_scales = mx_tiles("z2")
        quantize("z2_grouped", z2[:], z2_codes[:], z2_scales[:])
        product(b, w3_dealt, w3s_dealt, z2_codes, z2_scales)

        z = sbuf("z", [P, PACK, S], BF16)
        for t in range(PACK):
            pa = look_up("pa%d" % t, y[t], n1_sb, tag=ring() if t < LAST else "ring1")
            far = look_up("far%d" % t, y[t], n3_sb, tag=ring() if t < LAST else "z2_grouped")
            if t > 0:
                gate.append(look_up("gate%d" % t, y[t], n2_sb, ACT.Sigmoid, tag=ring() if t < LAST else "gate0"))
            step = sbuf("step%d" % t, [P, S], F32, tag="z2")
            nc.vector.tensor_tensor(step[:], far[:], pa[:], ALU.subtract)
            pull = sbuf("pull%d" % t, [P, S], F32)
            nc.vector.scalar_tensor_tensor(pull[:], step[:], gn_sb[:, t : t + 1], gate[t][:], ALU.mult, ALU.mult)
            nc.vector.scalar_tensor_tensor(z[:, t, :], pa[:], gn_sb[:, t : t + 1], pull[:], ALU.mult, ALU.add)
        z_codes, z_scales = mx_tiles("z")
        quantize("z_grouped", z[:], z_codes[:], z_scales[:])
        product(a, w2_dealt, w2s_dealt, z_codes, z_scales)

        out_rows = out_0.rearrange("(p t) c -> p t c", t=PACK)
        out_codes = out_1[0].rearrange("p c r -> p (c r)").bitcast(I32)
        result = sbuf("result", [P, PACK, S], F32)
        codes, scales = mx_tiles("out")
        b7 = []
        b8 = []
        for t in range(PACK):
            b7.append(look_up("b7_%d" % t, b[t], n7_sb))
            b8.append(look_up("b8_%d" % t, b[t], n8_sb))
        for t in range(LAST):
            a5 = look_up("a5_%d" % t, a[t], n5_sb)
            a6 = look_up("a6_%d" % t, a[t], n6_sb)
            first = add("first%d" % t, a5[:], b7[t][:])
            second = add("second%d" % t, a6[:], b8[t][:])
            nc.vector.tensor_tensor(result[:, t, :], first[:], second[:], ALU.max)
            nc.sync.dma_start(out_rows[:, t, :], result[:, t, :])
        a5 = look_up("a5_last", a[LAST], n5_sb)
        first = add("first_last", a5[:], b7[LAST][:])
        for c0, c1 in HALVES:
            a6 = look_up("a6_last%d" % c0, a[LAST], n6_sb, c0=c0, c1=c1)
            second = add("second_last%d" % c0, a6[:], b8[LAST][:, c0:c1])
            nc.vector.tensor_tensor(result[:, LAST, c0:c1], first[:, c0:c1], second[:], ALU.max)
            nc.sync.dma_start(out_rows[:, LAST, c0:c1], result[:, LAST, c0:c1])
            quantize("out_grouped%d" % c0, result[:, :, c0:c1], codes[:, c0:c1], scales[:, c0:c1])
            nc.sync.dma_start(out_codes[:, c0:c1], codes[:, c0:c1].bitcast(I32))
        for q in range(QUADS):
            queue = nc.sync if q % 2 else nc.scalar
            queue.dma_start(out_2[0, 4 * q : 4 * q + 4, :].bitcast(I32), scales[32 * q : 32 * q + 4, :].bitcast(I32))
